import numpy as np
import ml_dtypes


def mxq(x, axis, fmt="e4m3"):
    dtype, down = {"e4m3": (ml_dtypes.float8_e4m3fn, 7), "e5m2": (ml_dtypes.float8_e5m2, 14)}[fmt]
    v = np.moveaxis(np.asarray(x, np.float32).astype(ml_dtypes.bfloat16).astype(np.float64), axis, -1)
    blocks = v.reshape(v.shape[:-1] + (-1, 32))
    amax = np.abs(blocks).max(-1, keepdims=True)
    byte = np.maximum(np.where(amax > 0, np.frexp(amax)[1] - 1 + 127, 0) - down, 1)
    scale = np.exp2(byte - 127.0)
    codes = (blocks / scale).astype(np.float32).astype(dtype).astype(np.float64)
    return np.moveaxis((codes * scale).reshape(v.shape), -1, axis)


WIDE = False


def mx_kscale(k):
    if not WIDE:
        return np.ones(k)
    levels = np.array([10, -10, 5, -5, 0])
    if k % 512:
        return np.exp2(np.random.permutation(np.resize(levels, k // 32))).repeat(32)
    a = np.empty((k // 512, 16))
    for p in range(k // 512):
        a[p, :8] = np.random.permutation(np.resize(levels, 8))
        for g in range(8):
            far = levels[np.abs(levels - a[p, g]) >= 10]
            a[p, g + 8] = far[np.random.randint(len(far))]
    return np.exp2(a.ravel()).repeat(32)


def f64(x):
    return np.asarray(x).astype(np.float64)


def striped(idx):
    return np.tile(idx.reshape(-1, 16).T, (8, 1)).astype(np.uint16)


def unstriped(offs):
    return offs[:16].T.reshape(-1).astype(np.int64)


def pack_weight(w):
    k, n = w.shape
    w = f64(np.asarray(w, np.float32).astype(ml_dtypes.bfloat16)).reshape(k // 32, 32, n)
    amax = np.abs(w).max(1)
    byte = np.clip(np.where(amax > 0, np.frexp(amax)[1] - 1 + 127 - 7, 1), 1, 254)
    scaled = (w * np.exp2(127.0 - byte)[:, None, :]).reshape(k, n).astype(np.float32)
    words = np.ascontiguousarray(scaled.reshape(k // 512, 128, 4, n).transpose(0, 1, 3, 2)).astype(ml_dtypes.float8_e4m3fn).view(np.uint8)
    return words, np.ascontiguousarray(byte.astype(np.uint8).reshape(k // 512, 16, n))


def unpack_weight(words, scales):
    g, p, n, _ = words.shape
    vals = np.ascontiguousarray(words).view(ml_dtypes.float8_e4m3fn).astype(np.float64) * np.repeat(np.exp2(scales.astype(np.float64) - 127.0), 8, axis=1)[..., None]
    return vals.transpose(0, 1, 3, 2).reshape(g * 512, n)


K, T, S, V = 1024, 2048, 512, 512
P = 2 ** 7


def setup_inputs():
    n = np.random.standard_normal
    s = mx_kscale(K)[:, None]
    packed_xT = pack_weight(n((K, T)) * s)
    return {
        "x_words": packed_xT[0],
        "x_scales": packed_xT[1],
        "hT": (n((K, V)) / np.sqrt(K) / s).astype(np.float32),
        "cooc": (np.random.uniform(0.0, 1.0, (V, S)) ** 3 * 30 + 0.5).astype(np.float32),
        "cap": (np.tile(np.random.uniform(0.8, 1.0, S), (P, 1))).astype(np.float32),
        "ctxb": (np.tile(0.5 * n(T), (P, 1))).astype(np.float32),
        "tgtb": (0.5 * n((V, 1))).astype(np.float32),
        "offs": striped(np.random.permutation(T)[:S]),
    }


def reference(x_words, x_scales, hT, cooc, cap, ctxb, tgtb, offs):
    lx = np.log(f64(cooc))
    wt = np.minimum(np.exp(0.75 * (lx - 2.3)), f64(cap)[:1])
    hTq = mxq(f64(hT), 0, "e4m3")
    xq = unpack_weight(x_words, x_scales)[:, unstriped(offs)]
    y = hTq.T @ xq
    err = y + f64(ctxb)[:1][:, unstriped(offs)] - lx + f64(tgtb)
    ge = (wt * err) ** 2
    acc2 = ge.mean(axis=1, keepdims=True)
    return (wt * err) / np.sqrt(acc2 + 0.1)

@@ -1,0 +1,192 @@
+import math
+from contextlib import ExitStack
+
+import concourse.mybir as mybir
+from concourse.masks import make_identity
+
+K, T, S, V = 1024, 2048, 512, 512
+FLOPS = 2 * K * S * V
+BYTES = 2 * 128 * T * 4 + 2 * 16 * T + K * V * 4 + V * S * 4 + S * 4 + T * 4 + V * 4 + 128 * 32 * 2 + V * S * 4
+
+F32 = mybir.dt.float32
+BF16 = mybir.dt.bfloat16
+I32 = mybir.dt.int32
+U32 = mybir.dt.uint32
+U16 = mybir.dt.uint16
+U8 = mybir.dt.uint8
+FP8X4 = mybir.dt.float8_e4m3fn_x4
+ALU = mybir.AluOpType
+ACT = mybir.ActivationFunctionType
+
+P = 128
+PACK = 4
+PASSES = K // (P * PACK)
+BLOCKS = V // P
+HALF = V // 2
+PAD = 8
+
+
+def tile_picked_yglovw_ada_p_kernel(tc, x_words, x_scales, hT, cooc, cap, ctxb, tgtb, offs, out):
+    nc = tc.nc
+    with ExitStack() as ctx:
+        keep = ctx.enter_context(tc.tile_pool(name="keep", bufs=1))
+        psum = ctx.enter_context(tc.psum_pool(name="psum", bufs=1))
+
+        offsets = keep.tile([P, S // 16], U16, name="offsets")
+        nc.sync.dma_start(offsets[:], offs)
+
+        scale_window = keep.tile([P, T], U8, name="scale_window")
+        nc.gpsimd.memset(scale_window[:].bitcast(I32), 0)
+
+        ctx_window = keep.tile([P, T], F32, name="ctx_window")
+        nc.sync.dma_start(ctx_window[0:32, :], ctxb[0:32, :])
+        nc.vector.memset(ctx_window[32:64, :], 0.0)
+        nc.gpsimd.memset(ctx_window[64:P, :], 0.0)
+
+        cooc_rows = cooc.rearrange("(u e p) j -> e p u j", e=2, p=P)
+        counts = [keep.tile([P, 2, S], F32, name="counts%d" % e) for e in range(2)]
+        nc.sync.dma_start(counts[0][:], cooc_rows[0])
+        for q in range(4):
+            nc.sync.dma_start(
+                scale_window[32 * q : 32 * q + 4 * PASSES, :].bitcast(I32),
+                x_scales[:, 4 * q : 4 * q + 4, :].bitcast(I32),
+            )
+        nc.sync.dma_start(counts[1][:], cooc_rows[1])
+
+        word_windows = [keep.tile([P, T], U32, name="word_window%d" % o) for o in range(PASSES)]
+        word_rows = x_words.rearrange("o p n t -> o p (n t)")
+        nc.sync.dma_start(word_windows[0][:].bitcast(I32), word_rows[0].bitcast(I32))
+        rows = keep.tile([P, P], F32, name="rows")
+        nc.gpsimd.memset(rows[:], 0.0)
+        nc.sync.dma_start(rows[0:BLOCKS, :], cap[0:1, :].rearrange("o (b m) -> (o b) m", m=P))
+        nc.sync.dma_start(rows[BLOCKS : 2 * BLOCKS, :], tgtb.rearrange("(b m) o -> b (m o)", m=P))
+        nc.sync.dma_start(word_windows[1][:].bitcast(I32), word_rows[1].bitcast(I32))
+
+        raw = {}
+        for h in range(2):
+            for o in range(PASSES):
+                r = keep.tile([P, PACK, HALF], F32, name="raw%d%d" % (h, o))
+                src = hT[o * P * PACK : (o + 1) * P * PACK, h * HALF : (h + 1) * HALF]
+                nc.sync.dma_start(r[:], src.rearrange("(p j) c -> p j c", j=PACK))
+                raw[(h, o)] = r
+
+        ident = keep.tile([P, P], F32, name="ident")
+        make_identity(nc, ident[:])
+        minus_half = keep.tile([P, 1], F32, name="minus_half")
+        nc.gpsimd.memset(minus_half[:], -0.5)
+        one = keep.tile([P, BLOCKS], F32, name="one")
+        nc.gpsimd.memset(one[:], 1.0)
+        weighted = keep.tile([P, BLOCKS, S + PAD], F32, name="weighted")
+        nc.gpsimd.tensor_scalar(
+            out=weighted[:, :, S], in0=one[:], scalar1=math.sqrt(0.1 * S), scalar2=0.0, op0=ALU.mult, op1=ALU.add
+        )
+
+        ctx_picked = keep.tile([P, S], F32, name="ctx_picked")
+        nc.vector.tensor_copy(ctx_picked[:], ctx_window[:].indirect(offsets[:]))
+        x_scale = keep.tile([P, S], U8, name="x_scale", align_bytes=64)
+        nc.vector.tensor_copy(x_scale[:], scale_window[:].indirect(offsets[:]))
+
+        lx = keep.tile([P, 2, 2, S], F32, name="lx")
+        for e in range(2):
+            nc.scalar.activation(out=lx[:, :, e, :], in_=counts[e][:], func=ACT.Ln)
+
+        ctx_turned = psum.tile([P, S], F32, name="ctx_turned")
+        for b in range(BLOCKS):
+            nc.tensor.transpose(ctx_turned[:, b * P : (b + 1) * P], ctx_picked[:, b * P : (b + 1) * P], ident[:])
+        ctx_col = keep.tile([P, BLOCKS], F32, name="ctx_col")
+        nc.vector.tensor_copy(ctx_col[:], ctx_turned[:, 0:S:P])
+        ctx_all = psum.tile([P, S], F32, name="ctx_all")
+        for b in range(BLOCKS):
+            nc.tensor.transpose(ctx_all[:, b * P : (b + 1) * P], ctx_col[:, b : b + 1].to_broadcast([P, P]), ident[:])
+
+        rows_turned = psum.tile([P, P], F32, name="rows_turned")
+        nc.tensor.transpose(rows_turned[:], rows[:], ident[:])
+        cols = keep.tile([P, 2 * BLOCKS], F32, name="cols")
+        nc.vector.tensor_copy(cols[:], rows_turned[:, 0 : 2 * BLOCKS])
+        cap_all = psum.tile([P, S], F32, name="cap_all")
+        for b in range(BLOCKS):
+            nc.tensor.transpose(cap_all[:, b * P : (b + 1) * P], cols[:, b : b + 1].to_broadcast([P, P]), ident[:])
+
+        power = []
+        for u in range(2):
+            pw = keep.tile([P, 2, S], F32, name="power%d" % u)
+            nc.scalar.activation(out=pw[:], in_=lx[:, u, :, :], func=ACT.Exp, scale=0.75, bias=-0.75 * 2.3)
+            power.append(pw)
+
+        offset_terms = keep.tile([P, 2, 2, S], F32, name="offset_terms")
+        for e in range(2):
+            nc.vector.tensor_tensor(
+                out=offset_terms[:, :, e, :], in0=ctx_all[:].unsqueeze(1).to_broadcast([P, 2, S]),
+                in1=lx[:, :, e, :], op=ALU.subtract,
+            )
+
+        x_codes = []
+        for o in range(PASSES):
+            g = keep.tile([P, S], U32, name="x_codes%d" % o, align_bytes=64)
+            nc.vector.tensor_copy(g[:], word_windows[o][:].indirect(offsets[:]))
+            x_codes.append(g)
+
+        def quantise(h, o, c0, width):
+            tag = "%d%d%d" % (h, o, c0)
+            grouped = keep.tile([P, width, PACK], BF16, name="grouped" + tag, align_bytes=64)
+            nc.scalar.copy(
+                out=grouped[:].rearrange("p (c i) j -> p c j i", i=4),
+                in_=raw[(h, o)][:, :, c0 : c0 + width].rearrange("p j (c i) -> p c j i", i=4),
+            )
+            codes = keep.tile([P, width], U32, name="h_codes" + tag, align_bytes=64)
+            scale = keep.tile([P, width], U8, name="h_scale" + tag, align_bytes=64)
+            nc.vector.quantize_mx(
+                out=codes[:].bitcast(FP8X4), scales=scale[:], in_=grouped[:].rearrange("p c j -> p (c j)")
+            )
+            return [(codes[:, c : c + P], scale[:, c : c + P]) for c in range(0, width, P)]
+
+        ys = [psum.tile([P, S], F32, name="y%d" % b) for b in range(BLOCKS)]
+        for h in range(2):
+            for o in range(PASSES):
+                if o == PASSES - 1:
+                    parts = quantise(h, o, 0, P) + quantise(h, o, P, P)
+                else:
+                    parts = quantise(h, o, 0, HALF)
+                for e in range(2):
+                    h_codes, h_scale = parts[e]
+                    nc.tensor.matmul_mx(
+                        out=ys[2 * h + e][:],
+                        lhsT=h_codes.bitcast(FP8X4),
+                        lhsT_scale=h_scale,
+                        rhs=x_codes[o][:].bitcast(FP8X4),
+                        rhs_scale=x_scale[4 * o : P, :],
+                        start=(o == 0),
+                        stop=(o == PASSES - 1),
+                    )
+
+        weights = []
+        for u in range(2):
+            t = keep.tile([P, 2, S], F32, name="weight%d" % u)
+            nc.vector.tensor_tensor(
+                out=t[:], in0=cap_all[:].unsqueeze(1).to_broadcast([P, 2, S]), in1=power[u][:], op=ALU.min
+            )
+            weights.append(t)
+
+        for b in range(BLOCKS):
+            y = ys[b]
+            err = keep.tile([P, S], F32, name="err%d" % b)
+            nc.vector.scalar_tensor_tensor(
+                out=err[:], in0=y[:], scalar=cols[:, BLOCKS + b : BLOCKS + b + 1], in1=offset_terms[:, b // 2, b % 2, :],
+                op0=ALU.add, op1=ALU.add,
+            )
+            nc.vector.tensor_tensor(out=weighted[:, b, 0:S], in0=err[:], in1=weights[b // 2][:, b % 2, :], op=ALU.mult)
+            squares = keep.tile([P, S + 1], F32, name="squares%d" % b)
+            total = keep.tile([P, 1], F32, name="total%d" % b)
+            nc.scalar.activation(
+                out=squares[:], in_=weighted[:, b, 0 : S + 1], func=ACT.Square, scale=S**-0.5, accum_out=total[:]
+            )
+            factor = keep.tile([P, 1], F32, name="factor%d" % b)
+            nc.gpsimd.tensor_tensor(out=factor[:], in0=total[:], in1=minus_half[:], op=ALU.pow)
+            result = keep.tile([P, S], F32, name="result%d" % b)
+            if b == BLOCKS - 1:
+                nc.vector.tensor_scalar(
+                    out=result[:], in0=weighted[:, b, 0:S], scalar1=factor[:], scalar2=None, op0=ALU.mult
+                )
+            else:
+                nc.scalar.activation(out=result[:], in_=weighted[:, b, 0:S], func=ACT.Copy, scale=factor[:])
+            nc.sync.dma_start(out[b * P : (b + 1) * P, :], result[:])

@@ -23,7 +23,7 @@ PACK = 4
 PASSES = K // (P * PACK)
 BLOCKS = V // P
 HALF = V // 2
-PAD = 8
+PAD = 16
 
 
 def tile_picked_yglovw_ada_p_kernel(tc, x_words, x_scales, hT, cooc, cap, ctxb, tgtb, offs, out):
@@ -35,16 +35,25 @@ def tile_picked_yglovw_ada_p_kernel(tc, x_words, x_scales, hT, cooc, cap, ctxb, 
         offsets = keep.tile([P, S // 16], U16, name="offsets")
         nc.sync.dma_start(offsets[:], offs)
 
-        scale_window = keep.tile([P, T], U8, name="scale_window")
+        scale_window = keep.tile([P, T], U8, name="scale_window", align_bytes=256)
         nc.gpsimd.memset(scale_window[:].bitcast(I32), 0)
-
-        ctx_window = keep.tile([P, T], F32, name="ctx_window")
+        ctx_window = keep.tile([P, T], F32, name="ctx_window", align_bytes=256)
         nc.sync.dma_start(ctx_window[0:32, :], ctxb[0:32, :])
-        nc.vector.memset(ctx_window[32:64, :], 0.0)
-        nc.gpsimd.memset(ctx_window[64:P, :], 0.0)
+        nc.vector.memset(ctx_window[32:64, :].bitcast(I32), 0)
+        nc.vector.memset(ctx_window[64:P, :].bitcast(I32), 0)
+        ident = keep.tile([P, P], F32, name="ident")
+        make_identity(nc, ident[:])
+        one = keep.tile([P, 1], F32, name="one")
+        nc.gpsimd.memset(one[:], 1.0)
+        weighted = [keep.tile([P, S + PAD], F32, name="weighted%d" % b, align_bytes=64) for b in range(BLOCKS)]
+        for b in range(BLOCKS):
+            nc.gpsimd.tensor_scalar(
+                out=weighted[b][:, S : S + 1], in0=one[:], scalar1=math.sqrt(0.1 * S), scalar2=0.0,
+                op0=ALU.mult, op1=ALU.add,
+            )
 
         cooc_rows = cooc.rearrange("(u e p) j -> e p u j", e=2, p=P)
-        counts = [keep.tile([P, 2, S], F32, name="counts%d" % e) for e in range(2)]
+        counts = [keep.tile([P, 2, S], F32, name="counts%d" % e, align_bytes=256) for e in range(2)]
         nc.sync.dma_start(counts[0][:], cooc_rows[0])
         for q in range(4):
             nc.sync.dma_start(
@@ -53,7 +62,9 @@ def tile_picked_yglovw_ada_p_kernel(tc, x_words, x_scales, hT, cooc, cap, ctxb, 
             )
         nc.sync.dma_start(counts[1][:], cooc_rows[1])
 
-        word_windows = [keep.tile([P, T], U32, name="word_window%d" % o) for o in range(PASSES)]
+        word_windows = [
+            keep.tile([P, T], U32, name="word_window%d" % o, tag="words%d" % o, align_bytes=256) for o in range(PASSES)
+        ]
         word_rows = x_words.rearrange("o p n t -> o p (n t)")
         nc.sync.dma_start(word_windows[0][:].bitcast(I32), word_rows[0].bitcast(I32))
         rows = keep.tile([P, P], F32, name="rows")
@@ -62,24 +73,17 @@ def tile_picked_yglovw_ada_p_kernel(tc, x_words, x_scales, hT, cooc, cap, ctxb, 
         nc.sync.dma_start(rows[BLOCKS : 2 * BLOCKS, :], tgtb.rearrange("(b m) o -> b (m o)", m=P))
         nc.sync.dma_start(word_windows[1][:].bitcast(I32), word_rows[1].bitcast(I32))
 
+        pieces = [(0, 0, HALF), (1, 0, HALF), (0, HALF, HALF), (1, HALF, P), (1, HALF + P, P)]
         raw = {}
-        for h in range(2):
-            for o in range(PASSES):
-                r = keep.tile([P, PACK, HALF], F32, name="raw%d%d" % (h, o))
-                src = hT[o * P * PACK : (o + 1) * P * PACK, h * HALF : (h + 1) * HALF]
-                nc.sync.dma_start(r[:], src.rearrange("(p j) c -> p j c", j=PACK))
-                raw[(h, o)] = r
+        for o, t0, width in pieces:
+            flat = keep.tile([P, PACK * width + PAD], F32, name="raw%d_%d" % (o, t0), align_bytes=256)
+            raw[(o, t0)] = flat[:, 0 : PACK * width].rearrange("p (j c) -> p j c", j=PACK)
+            src = hT[o * P * PACK : (o + 1) * P * PACK, t0 : t0 + width]
+            nc.sync.dma_start(raw[(o, t0)], src.rearrange("(p j) c -> p j c", j=PACK))
+        squares = flat
 
-        ident = keep.tile([P, P], F32, name="ident")
-        make_identity(nc, ident[:])
         minus_half = keep.tile([P, 1], F32, name="minus_half")
         nc.gpsimd.memset(minus_half[:], -0.5)
-        one = keep.tile([P, BLOCKS], F32, name="one")
-        nc.gpsimd.memset(one[:], 1.0)
-        weighted = keep.tile([P, BLOCKS, S + PAD], F32, name="weighted")
-        nc.gpsimd.tensor_scalar(
-            out=weighted[:, :, S], in0=one[:], scalar1=math.sqrt(0.1 * S), scalar2=0.0, op0=ALU.mult, op1=ALU.add
-        )
 
         ctx_picked = keep.tile([P, S], F32, name="ctx_picked")
         nc.vector.tensor_copy(ctx_picked[:], ctx_window[:].indirect(offsets[:]))
@@ -93,9 +97,9 @@ def tile_picked_yglovw_ada_p_kernel(tc, x_words, x_scales, hT, cooc, cap, ctxb, 
         ctx_turned = psum.tile([P, S], F32, name="ctx_turned")
         for b in range(BLOCKS):
             nc.tensor.transpose(ctx_turned[:, b * P : (b + 1) * P], ctx_picked[:, b * P : (b + 1) * P], ident[:])
-        ctx_col = keep.tile([P, BLOCKS], F32, name="ctx_col")
+        ctx_col = keep.tile([P, BLOCKS], F32, name="ctx_col", tag="ctx_col", align_bytes=64)
         nc.vector.tensor_copy(ctx_col[:], ctx_turned[:, 0:S:P])
-        ctx_all = psum.tile([P, S], F32, name="ctx_all")
+        ctx_all = psum.tile([P, S], F32, name="ctx_all", tag="spread")
         for b in range(BLOCKS):
             nc.tensor.transpose(ctx_all[:, b * P : (b + 1) * P], ctx_col[:, b : b + 1].to_broadcast([P, P]), ident[:])
 
@@ -103,10 +107,6 @@ def tile_picked_yglovw_ada_p_kernel(tc, x_words, x_scales, hT, cooc, cap, ctxb, 
         nc.tensor.transpose(rows_turned[:], rows[:], ident[:])
         cols = keep.tile([P, 2 * BLOCKS], F32, name="cols")
         nc.vector.tensor_copy(cols[:], rows_turned[:, 0 : 2 * BLOCKS])
-        cap_all = psum.tile([P, S], F32, name="cap_all")
-        for b in range(BLOCKS):
-            nc.tensor.transpose(cap_all[:, b * P : (b + 1) * P], cols[:, b : b + 1].to_broadcast([P, P]), ident[:])
-
         power = []
         for u in range(2):
             pw = keep.tile([P, 2, S], F32, name="power%d" % u)
@@ -120,44 +120,47 @@ def tile_picked_yglovw_ada_p_kernel(tc, x_words, x_scales, hT, cooc, cap, ctxb, 
                 in1=lx[:, :, e, :], op=ALU.subtract,
             )
 
-        x_codes = []
+        cap_all = psum.tile([P, S], F32, name="cap_all", tag="spread")
+        for b in range(BLOCKS):
+            nc.tensor.transpose(cap_all[:, b * P : (b + 1) * P], cols[:, b : b + 1].to_broadcast([P, P]), ident[:])
+
+        x_codes = [
+            keep.tile([P, S], U32, name="x_codes0", tag="ctx_col", align_bytes=64),
+            keep.tile([P, S], U32, name="x_codes1", tag="words0", align_bytes=256),
+        ]
         for o in range(PASSES):
-            g = keep.tile([P, S], U32, name="x_codes%d" % o, align_bytes=64)
-            nc.vector.tensor_copy(g[:], word_windows[o][:].indirect(offsets[:]))
-            x_codes.append(g)
+            nc.vector.tensor_copy(x_codes[o][:], word_windows[o][:].indirect(offsets[:]))
 
-        def quantise(h, o, c0, width):
-            tag = "%d%d%d" % (h, o, c0)
-            grouped = keep.tile([P, width, PACK], BF16, name="grouped" + tag, align_bytes=64)
-            nc.scalar.copy(
-                out=grouped[:].rearrange("p (c i) j -> p c j i", i=4),
-                in_=raw[(h, o)][:, :, c0 : c0 + width].rearrange("p j (c i) -> p c j i", i=4),
-            )
-            codes = keep.tile([P, width], U32, name="h_codes" + tag, align_bytes=64)
-            scale = keep.tile([P, width], U8, name="h_scale" + tag, align_bytes=64)
-            nc.vector.quantize_mx(
-                out=codes[:].bitcast(FP8X4), scales=scale[:], in_=grouped[:].rearrange("p c j -> p (c j)")
-            )
-            return [(codes[:, c : c + P], scale[:, c : c + P]) for c in range(0, width, P)]
-
+        errs = [keep.tile([P, S], F32, name="err%d" % b, align_bytes=64) for b in range(BLOCKS)]
         ys = [psum.tile([P, S], F32, name="y%d" % b) for b in range(BLOCKS)]
-        for h in range(2):
-            for o in range(PASSES):
-                if o == PASSES - 1:
-                    parts = quantise(h, o, 0, P) + quantise(h, o, P, P)
-                else:
-                    parts = quantise(h, o, 0, HALF)
-                for e in range(2):
-                    h_codes, h_scale = parts[e]
-                    nc.tensor.matmul_mx(
-                        out=ys[2 * h + e][:],
-                        lhsT=h_codes.bitcast(FP8X4),
-                        lhsT_scale=h_scale,
-                        rhs=x_codes[o][:].bitcast(FP8X4),
-                        rhs_scale=x_scale[4 * o : P, :],
-                        start=(o == 0),
-                        stop=(o == PASSES - 1),
-                    )
+
+        def quantise(stage, o, t0, c0, width):
+            label = "%d_%d" % (o, t0 + c0)
+            grouped = stage[:, 0 : width * PACK // 2].bitcast(BF16)
+            nc.scalar.copy(
+                out=grouped.rearrange("p (c i j) -> p c j i", i=4, j=PACK),
+                in_=raw[(o, t0)][:, :, c0 : c0 + width].rearrange("p j (c i) -> p c j i", i=4),
+            )
+            codes = keep.tile([P, width], U32, name="h_codes" + label, align_bytes=64)
+            scale = keep.tile([P, width], U8, name="h_scale" + label, align_bytes=64)
+            nc.vector.quantize_mx(out=codes[:].bitcast(FP8X4), scales=scale[:], in_=grouped)
+            for c in range(0, width, P):
+                nc.tensor.matmul_mx(
+                    out=ys[(t0 + c0 + c) // P][:],
+                    lhsT=codes[:, c : c + P].bitcast(FP8X4),
+                    lhsT_scale=scale[:, c : c + P],
+                    rhs=x_codes[o][:].bitcast(FP8X4),
+                    rhs_scale=x_scale[4 * o : P, :],
+                    start=(o == 0),
+                    stop=(o == PASSES - 1),
+                )
+
+        quantise(weighted[0], 0, 0, 0, HALF)
+        quantise(weighted[3], 1, 0, 0, P)
+        quantise(errs[0], 1, 0, P, P)
+        quantise(errs[1], 0, HALF, 0, HALF)
+        quantise(weighted[1], 1, HALF, 0, P)
+        quantise(errs[2], 1, HALF + P, 0, P)
 
         weights = []
         for u in range(2):
@@ -168,25 +171,25 @@ def tile_picked_yglovw_ada_p_kernel(tc, x_words, x_scales, hT, cooc, cap, ctxb, 
             weights.append(t)
 
         for b in range(BLOCKS):
-            y = ys[b]
-            err = keep.tile([P, S], F32, name="err%d" % b)
             nc.vector.scalar_tensor_tensor(
-                out=err[:], in0=y[:], scalar=cols[:, BLOCKS + b : BLOCKS + b + 1], in1=offset_terms[:, b // 2, b % 2, :],
-                op0=ALU.add, op1=ALU.add,
+                out=errs[b][:], in0=ys[b][:], scalar=cols[:, BLOCKS + b : BLOCKS + b + 1],
+                in1=offset_terms[:, b // 2, b % 2, :], op0=ALU.add, op1=ALU.add,
             )
-            nc.vector.tensor_tensor(out=weighted[:, b, 0:S], in0=err[:], in1=weights[b // 2][:, b % 2, :], op=ALU.mult)
-            squares = keep.tile([P, S + 1], F32, name="squares%d" % b)
+            nc.vector.tensor_tensor(
+                out=weighted[b][:, 0:S], in0=errs[b][:], in1=weights[b // 2][:, b % 2, :], op=ALU.mult
+            )
             total = keep.tile([P, 1], F32, name="total%d" % b)
             nc.scalar.activation(
-                out=squares[:], in_=weighted[:, b, 0 : S + 1], func=ACT.Square, scale=S**-0.5, accum_out=total[:]
+                out=squares[:, 0 : S + 1], in_=weighted[b][:, 0 : S + 1], func=ACT.Square, scale=S**-0.5,
+                accum_out=total[:],
             )
             factor = keep.tile([P, 1], F32, name="factor%d" % b)
             nc.gpsimd.tensor_tensor(out=factor[:], in0=total[:], in1=minus_half[:], op=ALU.pow)
-            result = keep.tile([P, S], F32, name="result%d" % b)
-            if b == BLOCKS - 1:
+            result = keep.tile([P, S], F32, name="result%d" % b, align_bytes=256)
+            if b >= BLOCKS // 2:
                 nc.vector.tensor_scalar(
-                    out=result[:], in0=weighted[:, b, 0:S], scalar1=factor[:], scalar2=None, op0=ALU.mult
+                    out=result[:], in0=weighted[b][:, 0:S], scalar1=factor[:], scalar2=None, op0=ALU.mult
                 )
             else:
-                nc.scalar.activation(out=result[:], in_=weighted[:, b, 0:S], func=ACT.Copy, scale=factor[:])
+                nc.scalar.activation(out=result[:], in_=weighted[b][:, 0:S], func=ACT.Copy, scale=factor[:])
             nc.sync.dma_start(out[b * P : (b + 1) * P, :], result[:])

@@ -37,10 +37,11 @@ def tile_picked_yglovw_ada_p_kernel(tc, x_words, x_scales, hT, cooc, cap, ctxb, 
 
         scale_window = keep.tile([P, T], U8, name="scale_window", align_bytes=256)
         nc.gpsimd.memset(scale_window[:].bitcast(I32), 0)
-        ctx_window = keep.tile([P, T], F32, name="ctx_window", align_bytes=256)
+        ctx_window = keep.tile([P, T], F32, name="ctx_window", tag="ctx", align_bytes=256)
         nc.sync.dma_start(ctx_window[0:32, :], ctxb[0:32, :])
-        nc.vector.memset(ctx_window[32:64, :].bitcast(I32), 0)
-        nc.vector.memset(ctx_window[64:P, :].bitcast(I32), 0)
+        nc.vector.memset(ctx_window[32:64, 0 : T - 1], 0.0)
+        nc.vector.memset(ctx_window[32:64, T - 1 : T], 0.0)
+        nc.gpsimd.memset(ctx_window[64:P, :], 0.0)
         ident = keep.tile([P, P], F32, name="ident")
         make_identity(nc, ident[:])
         one = keep.tile([P, 1], F32, name="one")
@@ -71,7 +72,6 @@ def tile_picked_yglovw_ada_p_kernel(tc, x_words, x_scales, hT, cooc, cap, ctxb, 
         nc.gpsimd.memset(rows[:], 0.0)
         nc.sync.dma_start(rows[0:BLOCKS, :], cap[0:1, :].rearrange("o (b m) -> (o b) m", m=P))
         nc.sync.dma_start(rows[BLOCKS : 2 * BLOCKS, :], tgtb.rearrange("(b m) o -> b (m o)", m=P))
-        nc.sync.dma_start(word_windows[1][:].bitcast(I32), word_rows[1].bitcast(I32))
 
         pieces = [(0, 0, HALF), (1, 0, HALF), (0, HALF, HALF), (1, HALF, P), (1, HALF + P, P)]
         raw = {}
@@ -80,6 +80,8 @@ def tile_picked_yglovw_ada_p_kernel(tc, x_words, x_scales, hT, cooc, cap, ctxb, 
             raw[(o, t0)] = flat[:, 0 : PACK * width].rearrange("p (j c) -> p j c", j=PACK)
             src = hT[o * P * PACK : (o + 1) * P * PACK, t0 : t0 + width]
             nc.sync.dma_start(raw[(o, t0)], src.rearrange("(p j) c -> p j c", j=PACK))
+            if (o, t0) == pieces[0][0:2]:
+                nc.sync.dma_start(word_windows[1][:].bitcast(I32), word_rows[1].bitcast(I32))
         squares = flat
 
         minus_half = keep.tile([P, 1], F32, name="minus_half")
@@ -87,10 +89,10 @@ def tile_picked_yglovw_ada_p_kernel(tc, x_words, x_scales, hT, cooc, cap, ctxb, 
 
         ctx_picked = keep.tile([P, S], F32, name="ctx_picked")
         nc.vector.tensor_copy(ctx_picked[:], ctx_window[:].indirect(offsets[:]))
-        x_scale = keep.tile([P, S], U8, name="x_scale", align_bytes=64)
+        x_scale = keep.tile([P, S], U8, name="x_scale", tag="ctx", align_bytes=256)
         nc.vector.tensor_copy(x_scale[:], scale_window[:].indirect(offsets[:]))
 
-        lx = keep.tile([P, 2, 2, S], F32, name="lx")
+        lx = keep.tile([P, 2, 2, S], F32, name="lx", tag="logs", align_bytes=64)
         for e in range(2):
             nc.scalar.activation(out=lx[:, :, e, :], in_=counts[e][:], func=ACT.Ln)
 
@@ -109,7 +111,7 @@ def tile_picked_yglovw_ada_p_kernel(tc, x_words, x_scales, hT, cooc, cap, ctxb, 
         nc.vector.tensor_copy(cols[:], rows_turned[:, 0 : 2 * BLOCKS])
         power = []
         for u in range(2):
-            pw = keep.tile([P, 2, S], F32, name="power%d" % u)
+            pw = keep.tile([P, 2, S], F32, name="power%d" % u, tag="power%d" % u, align_bytes=64)
             nc.scalar.activation(out=pw[:], in_=lx[:, u, :, :], func=ACT.Exp, scale=0.75, bias=-0.75 * 2.3)
             power.append(pw)
 
@@ -120,29 +122,25 @@ def tile_picked_yglovw_ada_p_kernel(tc, x_words, x_scales, hT, cooc, cap, ctxb, 
                 in1=lx[:, :, e, :], op=ALU.subtract,
             )
 
-        cap_all = psum.tile([P, S], F32, name="cap_all", tag="spread")
+        cap_all = psum.tile([P, S], F32, name="cap_all")
         for b in range(BLOCKS):
             nc.tensor.transpose(cap_all[:, b * P : (b + 1) * P], cols[:, b : b + 1].to_broadcast([P, P]), ident[:])
 
-        x_codes = [
-            keep.tile([P, S], U32, name="x_codes0", tag="ctx_col", align_bytes=64),
-            keep.tile([P, S], U32, name="x_codes1", tag="words0", align_bytes=256),
-        ]
-        for o in range(PASSES):
-            nc.vector.tensor_copy(x_codes[o][:], word_windows[o][:].indirect(offsets[:]))
+        x_codes = [keep.tile([P, S], U32, name="x_codes0", tag="ctx_col", align_bytes=64)]
+        nc.vector.tensor_copy(x_codes[0][:], word_windows[0][:].indirect(offsets[:]))
 
         errs = [keep.tile([P, S], F32, name="err%d" % b, align_bytes=64) for b in range(BLOCKS)]
         ys = [psum.tile([P, S], F32, name="y%d" % b) for b in range(BLOCKS)]
 
-        def quantise(stage, o, t0, c0, width):
+        def quantise(stage, o, t0, c0, width, slot=None):
             label = "%d_%d" % (o, t0 + c0)
-            grouped = stage[:, 0 : width * PACK // 2].bitcast(BF16)
+            grouped = stage.bitcast(BF16)
             nc.scalar.copy(
                 out=grouped.rearrange("p (c i j) -> p c j i", i=4, j=PACK),
                 in_=raw[(o, t0)][:, :, c0 : c0 + width].rearrange("p j (c i) -> p c j i", i=4),
             )
             codes = keep.tile([P, width], U32, name="h_codes" + label, align_bytes=64)
-            scale = keep.tile([P, width], U8, name="h_scale" + label, align_bytes=64)
+            scale = keep.tile([P, width], U8, name="h_scale" + label, tag=slot or label, align_bytes=64)
             nc.vector.quantize_mx(out=codes[:].bitcast(FP8X4), scales=scale[:], in_=grouped)
             for c in range(0, width, P):
                 nc.tensor.matmul_mx(
@@ -155,22 +153,28 @@ def tile_picked_yglovw_ada_p_kernel(tc, x_words, x_scales, hT, cooc, cap, ctxb, 
                     stop=(o == PASSES - 1),
                 )
 
-        quantise(weighted[0], 0, 0, 0, HALF)
-        quantise(weighted[3], 1, 0, 0, P)
-        quantise(errs[0], 1, 0, P, P)
-        quantise(errs[1], 0, HALF, 0, HALF)
-        quantise(weighted[1], 1, HALF, 0, P)
-        quantise(errs[2], 1, HALF + P, 0, P)
-
-        weights = []
-        for u in range(2):
-            t = keep.tile([P, 2, S], F32, name="weight%d" % u)
+        def capped(u, slot):
+            t = keep.tile([P, 2, S], F32, name="weight%d" % u, tag=slot, align_bytes=256)
             nc.vector.tensor_tensor(
                 out=t[:], in0=cap_all[:].unsqueeze(1).to_broadcast([P, 2, S]), in1=power[u][:], op=ALU.min
             )
-            weights.append(t)
+            return t
 
-        for b in range(BLOCKS):
+        weights = [capped(0, "weight0")]
+        first_stage = keep.tile([P, S], F32, name="first_stage", tag="logs", align_bytes=64)
+        quantise(first_stage[:], 0, 0, 0, HALF)
+        x_codes.append(keep.tile([P, S], U32, name="x_codes1", tag="logs", align_bytes=64))
+        nc.vector.tensor_copy(x_codes[1][:], word_windows[1][:].indirect(offsets[:]))
+        quantise(weighted[3][:, 0:HALF], 1, 0, 0, P)
+        quantise(weighted[3][:, HALF:S], 1, 0, P, P)
+        weights.append(capped(1, "words1"))
+        quantise(errs[0][:, 0:S], 0, HALF, 0, HALF, "power1")
+        quantise(errs[1][:, 0:HALF], 1, HALF, 0, P)
+        quantise(errs[1][:, HALF:S], 1, HALF + P, 0, P)
+
+        errs_wide = keep.tile([P, S + PAD], F32, name="errs_wide")
+
+        def weigh(b):
             nc.vector.scalar_tensor_tensor(
                 out=errs[b][:], in0=ys[b][:], scalar=cols[:, BLOCKS + b : BLOCKS + b + 1],
                 in1=offset_terms[:, b // 2, b % 2, :], op0=ALU.add, op1=ALU.add,
@@ -178,14 +182,25 @@ def tile_picked_yglovw_ada_p_kernel(tc, x_words, x_scales, hT, cooc, cap, ctxb, 
             nc.vector.tensor_tensor(
                 out=weighted[b][:, 0:S], in0=errs[b][:], in1=weights[b // 2][:, b % 2, :], op=ALU.mult
             )
+
+        def normalise(b):
             total = keep.tile([P, 1], F32, name="total%d" % b)
-            nc.scalar.activation(
-                out=squares[:, 0 : S + 1], in_=weighted[b][:, 0 : S + 1], func=ACT.Square, scale=S**-0.5,
-                accum_out=total[:],
-            )
+            padded = weighted[b][:, 0 : S + 1]
+            if b == BLOCKS - 1:
+                nc.vector.scalar_tensor_tensor(
+                    out=errs_wide[:, 0 : S + 1], in0=padded, scalar=1.0 / S, in1=padded, op0=ALU.mult, op1=ALU.mult,
+                    accum_out=total[:],
+                )
+            else:
+                nc.scalar.activation(
+                    out=squares[:, 0 : S + 1], in_=padded, func=ACT.Square, scale=S**-0.5, accum_out=total[:]
+                )
             factor = keep.tile([P, 1], F32, name="factor%d" % b)
             nc.gpsimd.tensor_tensor(out=factor[:], in0=total[:], in1=minus_half[:], op=ALU.pow)
-            result = keep.tile([P, S], F32, name="result%d" % b, align_bytes=256)
+            if b == BLOCKS - 2:
+                result = errs[BLOCKS - 1]
+            else:
+                result = keep.tile([P, S], F32, name="result%d" % b, align_bytes=256)
             if b >= BLOCKS // 2:
                 nc.vector.tensor_scalar(
                     out=result[:], in0=weighted[b][:, 0:S], scalar1=factor[:], scalar2=None, op0=ALU.mult
@@ -193,3 +208,9 @@ def tile_picked_yglovw_ada_p_kernel(tc, x_words, x_scales, hT, cooc, cap, ctxb, 
             else:
                 nc.scalar.activation(out=result[:], in_=weighted[b][:, 0:S], func=ACT.Copy, scale=factor[:])
             nc.sync.dma_start(out[b * P : (b + 1) * P, :], result[:])
+
+        weigh(0)
+        for b in range(BLOCKS):
+            if b + 1 < BLOCKS:
+                weigh(b + 1)
+            normalise(b)

@@ -136,8 +136,8 @@ def tile_picked_yglovw_ada_p_kernel(tc, x_words, x_scales, hT, cooc, cap, ctxb, 
             label = "%d_%d" % (o, t0 + c0)
             grouped = stage.bitcast(BF16)
             nc.scalar.copy(
-                out=grouped.rearrange("p (c i j) -> p c j i", i=4, j=PACK),
-                in_=raw[(o, t0)][:, :, c0 : c0 + width].rearrange("p j (c i) -> p c j i", i=4),
+                out=grouped.rearrange("p (c j) -> p c j", j=PACK),
+                in_=raw[(o, t0)][:, :, c0 : c0 + width].rearrange("p j c -> p c j"),
             )
             codes = keep.tile([P, width], U32, name="h_codes" + label, align_bytes=64)
             scale = keep.tile([P, width], U8, name="h_scale" + label, tag=slot or label, align_bytes=64)
@@ -172,7 +172,7 @@ def tile_picked_yglovw_ada_p_kernel(tc, x_words, x_scales, hT, cooc, cap, ctxb, 
         quantise(errs[1][:, 0:HALF], 1, HALF, 0, P)
         quantise(errs[1][:, HALF:S], 1, HALF + P, 0, P)
 
-        errs_wide = keep.tile([P, S + PAD], F32, name="errs_wide")
+        errs_wide = keep.tile([P, S + PAD], F32, name="errs_wide", align_bytes=256)
 
         def weigh(b):
             nc.vector.scalar_tensor_tensor(
@@ -183,7 +183,7 @@ def tile_picked_yglovw_ada_p_kernel(tc, x_words, x_scales, hT, cooc, cap, ctxb, 
                 out=weighted[b][:, 0:S], in0=errs[b][:], in1=weights[b // 2][:, b % 2, :], op=ALU.mult
             )
 
-        def normalise(b):
+        def row_factor(b):
             total = keep.tile([P, 1], F32, name="total%d" % b)
             padded = weighted[b][:, 0 : S + 1]
             if b == BLOCKS - 1:
@@ -197,20 +197,24 @@ def tile_picked_yglovw_ada_p_kernel(tc, x_words, x_scales, hT, cooc, cap, ctxb, 
                 )
             factor = keep.tile([P, 1], F32, name="factor%d" % b)
             nc.gpsimd.tensor_tensor(out=factor[:], in0=total[:], in1=minus_half[:], op=ALU.pow)
+            return factor
+
+        def normalise(b, factor):
             if b == BLOCKS - 2:
-                result = errs[BLOCKS - 1]
+                result = errs_wide
             else:
                 result = keep.tile([P, S], F32, name="result%d" % b, align_bytes=256)
             if b >= BLOCKS // 2:
                 nc.vector.tensor_scalar(
-                    out=result[:], in0=weighted[b][:, 0:S], scalar1=factor[:], scalar2=None, op0=ALU.mult
+                    out=result[:, 0:S], in0=weighted[b][:, 0:S], scalar1=factor[:], scalar2=None, op0=ALU.mult
                 )
             else:
-                nc.scalar.activation(out=result[:], in_=weighted[b][:, 0:S], func=ACT.Copy, scale=factor[:])
-            nc.sync.dma_start(out[b * P : (b + 1) * P, :], result[:])
+                nc.scalar.activation(out=result[:, 0:S], in_=weighted[b][:, 0:S], func=ACT.Copy, scale=factor[:])
+            nc.sync.dma_start(out[b * P : (b + 1) * P, :], result[:, 0:S])
 
-        weigh(0)
+        factors = []
         for b in range(BLOCKS):
-            if b + 1 < BLOCKS:
-                weigh(b + 1)
-            normalise(b)
+            weigh(b)
+            factors.append(row_factor(b))
+        for b in range(BLOCKS):
+            normalise(b, factors[b])

import math
from contextlib import ExitStack

import concourse.mybir as mybir
from concourse.masks import make_identity

K, T, S, V = 1024, 2048, 512, 512
FLOPS = 2 * K * S * V
BYTES = 2 * 128 * T * 4 + 2 * 16 * T + K * V * 4 + V * S * 4 + S * 4 + T * 4 + V * 4 + 128 * 32 * 2 + V * S * 4

F32 = mybir.dt.float32
BF16 = mybir.dt.bfloat16
I32 = mybir.dt.int32
U32 = mybir.dt.uint32
U16 = mybir.dt.uint16
U8 = mybir.dt.uint8
FP8X4 = mybir.dt.float8_e4m3fn_x4
ALU = mybir.AluOpType
ACT = mybir.ActivationFunctionType

P = 128
PACK = 4
PASSES = K // (P * PACK)
BLOCKS = V // P
HALF = V // 2
PAD = 16


def tile_picked_yglovw_ada_p_kernel(tc, x_words, x_scales, hT, cooc, cap, ctxb, tgtb, offs, out):
    nc = tc.nc
    with ExitStack() as ctx:
        keep = ctx.enter_context(tc.tile_pool(name="keep", bufs=1))
        psum = ctx.enter_context(tc.psum_pool(name="psum", bufs=1))

        offsets = keep.tile([P, S // 16], U16, name="offsets")
        nc.sync.dma_start(offsets[:], offs)

        scale_window = keep.tile([P, T], U8, name="scale_window", align_bytes=256)
        nc.gpsimd.memset(scale_window[:].bitcast(I32), 0)
        ctx_window = keep.tile([P, T], F32, name="ctx_window", tag="ctx", align_bytes=256)
        nc.sync.dma_start(ctx_window[0:32, :], ctxb[0:32, :])
        nc.vector.memset(ctx_window[32:64, 0 : T - 1], 0.0)
        nc.vector.memset(ctx_window[32:64, T - 1 : T], 0.0)
        nc.gpsimd.memset(ctx_window[64:P, :], 0.0)
        ident = keep.tile([P, P], F32, name="ident")
        make_identity(nc, ident[:])
        one = keep.tile([P, 1], F32, name="one")
        nc.gpsimd.memset(one[:], 1.0)
        weighted = [keep.tile([P, S + PAD], F32, name="weighted%d" % b, align_bytes=64) for b in range(BLOCKS)]
        for b in range(BLOCKS):
            nc.gpsimd.tensor_scalar(
                out=weighted[b][:, S : S + 1], in0=one[:], scalar1=math.sqrt(0.1 * S), scalar2=0.0,
                op0=ALU.mult, op1=ALU.add,
            )

        cooc_rows = cooc.rearrange("(u e p) j -> e p u j", e=2, p=P)
        counts = [keep.tile([P, 2, S], F32, name="counts%d" % e, align_bytes=256) for e in range(2)]
        nc.sync.dma_start(counts[0][:], cooc_rows[0])
        for q in range(4):
            nc.sync.dma_start(
                scale_window[32 * q : 32 * q + 4 * PASSES, :].bitcast(I32),
                x_scales[:, 4 * q : 4 * q + 4, :].bitcast(I32),
            )
        nc.sync.dma_start(counts[1][:], cooc_rows[1])

        word_windows = [
            keep.tile([P, T], U32, name="word_window%d" % o, tag="words%d" % o, align_bytes=256) for o in range(PASSES)
        ]
        word_rows = x_words.rearrange("o p n t -> o p (n t)")
        nc.sync.dma_start(word_windows[0][:].bitcast(I32), word_rows[0].bitcast(I32))
        rows = keep.tile([P, P], F32, name="rows")
        nc.gpsimd.memset(rows[:], 0.0)
        nc.sync.dma_start(rows[0:BLOCKS, :], cap[0:1, :].rearrange("o (b m) -> (o b) m", m=P))
        nc.sync.dma_start(rows[BLOCKS : 2 * BLOCKS, :], tgtb.rearrange("(b m) o -> b (m o)", m=P))

        pieces = [(0, 0, HALF), (1, 0, HALF), (0, HALF, HALF), (1, HALF, P), (1, HALF + P, P)]
        raw = {}
        for o, t0, width in pieces:
            flat = keep.tile([P, PACK * width + PAD], F32, name="raw%d_%d" % (o, t0), align_bytes=256)
            raw[(o, t0)] = flat[:, 0 : PACK * width].rearrange("p (j c) -> p j c", j=PACK)
            src = hT[o * P * PACK : (o + 1) * P * PACK, t0 : t0 + width]
            nc.sync.dma_start(raw[(o, t0)], src.rearrange("(p j) c -> p j c", j=PACK))
            if (o, t0) == pieces[0][0:2]:
                nc.sync.dma_start(word_windows[1][:].bitcast(I32), word_rows[1].bitcast(I32))
        squares = flat

        minus_half = keep.tile([P, 1], F32, name="minus_half")
        nc.gpsimd.memset(minus_half[:], -0.5)

        ctx_picked = keep.tile([P, S], F32, name="ctx_picked")
        nc.vector.tensor_copy(ctx_picked[:], ctx_window[:].indirect(offsets[:]))
        x_scale = keep.tile([P, S], U8, name="x_scale", tag="ctx", align_bytes=256)
        nc.vector.tensor_copy(x_scale[:], scale_window[:].indirect(offsets[:]))

        lx = keep.tile([P, 2, 2, S], F32, name="lx", tag="logs", align_bytes=64)
        for e in range(2):
            nc.scalar.activation(out=lx[:, :, e, :], in_=counts[e][:], func=ACT.Ln)

        ctx_turned = psum.tile([P, S], F32, name="ctx_turned")
        for b in range(BLOCKS):
            nc.tensor.transpose(ctx_turned[:, b * P : (b + 1) * P], ctx_picked[:, b * P : (b + 1) * P], ident[:])
        ctx_col = keep.tile([P, BLOCKS], F32, name="ctx_col", tag="ctx_col", align_bytes=64)
        nc.vector.tensor_copy(ctx_col[:], ctx_turned[:, 0:S:P])
        ctx_all = psum.tile([P, S], F32, name="ctx_all", tag="spread")
        for b in range(BLOCKS):
            nc.tensor.transpose(ctx_all[:, b * P : (b + 1) * P], ctx_col[:, b : b + 1].to_broadcast([P, P]), ident[:])

        rows_turned = psum.tile([P, P], F32, name="rows_turned")
        nc.tensor.transpose(rows_turned[:], rows[:], ident[:])
        cols = keep.tile([P, 2 * BLOCKS], F32, name="cols")
        nc.vector.tensor_copy(cols[:], rows_turned[:, 0 : 2 * BLOCKS])
        power = []
        for u in range(2):
            pw = keep.tile([P, 2, S], F32, name="power%d" % u, tag="power%d" % u, align_bytes=64)
            nc.scalar.activation(out=pw[:], in_=lx[:, u, :, :], func=ACT.Exp, scale=0.75, bias=-0.75 * 2.3)
            power.append(pw)

        offset_terms = keep.tile([P, 2, 2, S], F32, name="offset_terms")
        for e in range(2):
            nc.vector.tensor_tensor(
                out=offset_terms[:, :, e, :], in0=ctx_all[:].unsqueeze(1).to_broadcast([P, 2, S]),
                in1=lx[:, :, e, :], op=ALU.subtract,
            )

        cap_all = psum.tile([P, S], F32, name="cap_all")
        for b in range(BLOCKS):
            nc.tensor.transpose(cap_all[:, b * P : (b + 1) * P], cols[:, b : b + 1].to_broadcast([P, P]), ident[:])

        x_codes = [keep.tile([P, S], U32, name="x_codes0", tag="ctx_col", align_bytes=64)]
        nc.vector.tensor_copy(x_codes[0][:], word_windows[0][:].indirect(offsets[:]))

        errs = [keep.tile([P, S], F32, name="err%d" % b, align_bytes=64) for b in range(BLOCKS)]
        ys = [psum.tile([P, S], F32, name="y%d" % b) for b in range(BLOCKS)]

        def quantise(stage, o, t0, c0, width, slot=None):
            label = "%d_%d" % (o, t0 + c0)
            grouped = stage.bitcast(BF16)
            nc.scalar.copy(
                out=grouped.rearrange("p (c j) -> p c j", j=PACK),
                in_=raw[(o, t0)][:, :, c0 : c0 + width].rearrange("p j c -> p c j"),
            )
            codes = keep.tile([P, width], U32, name="h_codes" + label, align_bytes=64)
            scale = keep.tile([P, width], U8, name="h_scale" + label, tag=slot or label, align_bytes=64)
            nc.vector.quantize_mx(out=codes[:].bitcast(FP8X4), scales=scale[:], in_=grouped)
            for c in range(0, width, P):
                nc.tensor.matmul_mx(
                    out=ys[(t0 + c0 + c) // P][:],
                    lhsT=codes[:, c : c + P].bitcast(FP8X4),
                    lhsT_scale=scale[:, c : c + P],
                    rhs=x_codes[o][:].bitcast(FP8X4),
                    rhs_scale=x_scale[4 * o : P, :],
                    start=(o == 0),
                    stop=(o == PASSES - 1),
                )

        def capped(u, slot):
            t = keep.tile([P, 2, S], F32, name="weight%d" % u, tag=slot, align_bytes=256)
            nc.vector.tensor_tensor(
                out=t[:], in0=cap_all[:].unsqueeze(1).to_broadcast([P, 2, S]), in1=power[u][:], op=ALU.min
            )
            return t

        weights = [capped(0, "weight0")]
        first_stage = keep.tile([P, S], F32, name="first_stage", tag="logs", align_bytes=64)
        quantise(first_stage[:], 0, 0, 0, HALF)
        x_codes.append(keep.tile([P, S], U32, name="x_codes1", tag="logs", align_bytes=64))
        nc.vector.tensor_copy(x_codes[1][:], word_windows[1][:].indirect(offsets[:]))
        quantise(weighted[3][:, 0:HALF], 1, 0, 0, P)
        quantise(weighted[3][:, HALF:S], 1, 0, P, P)
        weights.append(capped(1, "words1"))
        quantise(errs[0][:, 0:S], 0, HALF, 0, HALF, "power1")
        quantise(errs[1][:, 0:HALF], 1, HALF, 0, P)
        quantise(errs[1][:, HALF:S], 1, HALF + P, 0, P)

        errs_wide = keep.tile([P, S + PAD], F32, name="errs_wide", align_bytes=256)

        def weigh(b):
            nc.vector.scalar_tensor_tensor(
                out=errs[b][:], in0=ys[b][:], scalar=cols[:, BLOCKS + b : BLOCKS + b + 1],
                in1=offset_terms[:, b // 2, b % 2, :], op0=ALU.add, op1=ALU.add,
            )
            nc.vector.tensor_tensor(
                out=weighted[b][:, 0:S], in0=errs[b][:], in1=weights[b // 2][:, b % 2, :], op=ALU.mult
            )

        def row_factor(b):
            total = keep.tile([P, 1], F32, name="total%d" % b)
            padded = weighted[b][:, 0 : S + 1]
            if b == BLOCKS - 1:
                nc.vector.scalar_tensor_tensor(
                    out=errs_wide[:, 0 : S + 1], in0=padded, scalar=1.0 / S, in1=padded, op0=ALU.mult, op1=ALU.mult,
                    accum_out=total[:],
                )
            else:
                nc.scalar.activation(
                    out=squares[:, 0 : S + 1], in_=padded, func=ACT.Square, scale=S**-0.5, accum_out=total[:]
                )
            factor = keep.tile([P, 1], F32, name="factor%d" % b)
            nc.gpsimd.tensor_tensor(out=factor[:], in0=total[:], in1=minus_half[:], op=ALU.pow)
            return factor

        def normalise(b, factor):
            if b == BLOCKS - 2:
                result = errs_wide
            else:
                result = keep.tile([P, S], F32, name="result%d" % b, align_bytes=256)
            if b >= BLOCKS // 2:
                nc.vector.tensor_scalar(
                    out=result[:, 0:S], in0=weighted[b][:, 0:S], scalar1=factor[:], scalar2=None, op0=ALU.mult
                )
            else:
                nc.scalar.activation(out=result[:, 0:S], in_=weighted[b][:, 0:S], func=ACT.Copy, scale=factor[:])
            nc.sync.dma_start(out[b * P : (b + 1) * P, :], result[:, 0:S])

        factors = []
        for b in range(BLOCKS):
            weigh(b)
            factors.append(row_factor(b))
        for b in range(BLOCKS):
            normalise(b, factors[b])
